import numpy as np, ml_dtypes
CORES = [16,17,18,19,32,33,34,35]
N = 8
BF = ml_dtypes.bfloat16
def gentries(a):
    return np.ascontiguousarray(a.reshape(8, 16, -1).transpose(0, 2, 1)).reshape(8, -1)
def gtable(e):
    e = np.asarray(e); return np.ascontiguousarray(e.reshape(8, -1, 16).transpose(0, 2, 1)).reshape(128, -1).astype(np.int32)
W, UN, P, SH, MS = 8192, 192, 16, 4, (1, 2)
def parts(rng):
    e = (0.5 + 2.5 * rng.random((N, 8, 16, 1))).astype(np.float32)
    sh = np.minimum(np.floor(256 * rng.random((N, 8, 16, W), dtype=np.float32) ** e), 255)
    return sh, rng.integers(0, W, (N, 8, UN, P))
def pack(sh, un):
    return {"shelf": np.ascontiguousarray(sh.reshape(N, 128, W)).astype(np.float32).astype(BF), "units": np.stack([gtable(a.reshape(8, -1)) for a in un])}
def setup_inputs(rng):
    sh, un = parts(rng)
    return pack(sh, un)
def setup_inputs_ties(rng):
    sh, un = parts(rng)
    sh = (rng.random((N, 8, 16, W)) < 0.03) * rng.choice(np.array([1, 7, 255]), (1, 8, 1, 1))
    sh[:, rng.integers(0, 8)] = 9
    return pack(sh, un)
def setup_inputs_alike(rng):
    sh, un = parts(rng)
    un[:, 0] = un[0, 0].copy()
    un[:, 1] = rng.choice(np.array([0, 1, W - 1, W // 2]), (N, UN, P))
    un[:, 2] = un[:, 2, :1].copy()
    un[:, 3] = un[:, 3, :, :1].copy()
    un[:, 4] = 0
    un[:, 5, 1::2] = un[:, 5, ::2].copy()
    un[:, 6, :, P // 2:] = un[:1, 6, :1, P // 2:].copy()
    return pack(sh, un)
def setup_inputs_ends(rng):
    sh, un = parts(rng)
    sh[:, :7] = sh[:1, :7].copy(); x = rng.integers(1, W, (N, 7, UN)); un[:, :7] = 0
    for g, e in enumerate((0, P - 1, P // 2 - 1, P // 2, 1, P - 2, int(rng.integers(0, P)))): un[:, g, :, e] = x[:, g]
    return pack(sh, un)
def setup_inputs_rare(rng):
    sh, un = parts(rng)
    few = W // (8 * P) * np.array([1, 2, 3, 4, 2, 3])[:, None, None]
    hit = np.argsort(rng.random((N, 6, 1, W)), axis=-1) < few
    v = rng.integers(1, 256, (N, 6, 16, W)); v[:, 0] = 1; v[:, 1] = 255
    v = np.where(hit, v, 0); v[:, 4:] = 255 - v[:, 4:]
    sh[:, :6] = v
    sh[:, 6] = rng.choice(np.array([0, 1, 2, 253, 254, 255]), (N, 16, W))
    sh[:, 7] = np.clip(rng.integers(-64, 320, (N, 16, W)), 0, 255)
    sh = np.where((sh == 0) & (rng.random(sh.shape, dtype=np.float32) < 0.5), np.float32(-0.0), sh)
    return pack(sh, un)
def setup_inputs_spread(rng):
    sh, un = parts(rng)
    k = np.exp2(8 * rng.random((N, 8, 1, W))) * (rng.random((N, 8, 1, W)) > 0.0625)
    sh = np.minimum(np.floor(rng.random((N, 8, 16, W)) * k), 255)
    un = np.minimum((W * rng.random((N, 8, UN, P)) ** rng.choice(np.array([1, 2, 4, 8]), (N, 8, 1, 1))).astype(np.int64), W - 1)
    return pack(sh, un)
def check_inputs(d):
    bad = []; v = np.asarray(d["shelf"]).astype(np.float32)
    if not np.all((v >= 0) & (v <= 255) & (v == np.floor(v))): bad.append("values of shelf")
    if np.min(d["units"]) < 0 or np.max(d["units"]) > W - 1: bad.append("range of units")
    return bad
def reference(shelf, units):
    tab = np.ascontiguousarray(shelf.astype(np.float32).astype(np.int16).reshape(N, 8, 16, W).transpose(0, 1, 3, 2))
    un = np.stack([gentries(a) for a in units]).astype(np.int64).reshape(N, 8, UN, P)
    A = np.zeros((N, 8), np.int64); rank = np.arange(N); place = np.arange(P)
    n3, g3 = rank[:, None, None], np.arange(8)[None, :, None]
    def measure(x):
        z = (A[:, :, None, None] + np.add.accumulate(x, axis=3)) & 4095
        c = ((z * z >> SH) + x) & (W - 1)
        b = tab[n3[..., None], g3[..., None], c]
        return np.sum((np.max(b, axis=3) - np.min(b, axis=3)).astype(np.int64), axis=3)
    for m in MS:
        mate = rank ^ m; low = (rank < mate)[:, None, None]
        q = measure(un)
        order = np.argsort(np.where(low, -q, q), axis=2, kind="stable")
        own = un[n3, g3, order]; qo = q[n3, g3, order]; far = own[mate]; qf = qo[mate]
        s0 = np.where(low, qo > qf, qf > qo)
        first = np.zeros((N, 8, UN), np.int64); n = P
        while n > 1:
            n = n // 2
            swapped = (place >= first[..., None]) & (place < first[..., None] + n)
            a = measure(np.where(swapped, far, own)); b = a[mate]
            s = np.where(low, a > b, b > a)
            first = np.where(s != s0, first, first + n)
        takes = np.where(low, qo < qf, qo <= qf)
        new = np.where(takes[..., None] & (place == first[..., None]), far, own)
        un = np.zeros_like(un); un[n3, g3, order] = new
        A = np.sum(first, axis=2)
    return {"yu": np.stack([gtable(a.reshape(8, -1)) for a in un]).astype(np.float32), "yq": q.astype(np.float32)}

@@ -1,0 +1,588 @@
+from concourse.bass import DstId, RemoteDMATransfer
+from concourse.mybir import AluOpType, AxisListType, ActivationFunctionType
+
+ALU = AluOpType
+ACT = ActivationFunctionType
+BIG = float(1 << 19)
+NC = 3
+CW = 64
+EW = CW * 16
+VG = 32
+UN = 192
+
+SCRATCH = {}
+GRAN = {}
+
+
+def _buf(names, cols, dtype, gran=None, where="sbuf"):
+    for name in names.split():
+        SCRATCH[name] = (where, [128, cols], dtype)
+        GRAN[name] = gran if gran else cols
+
+
+_buf("U32", UN, "int32")
+_buf("U16 Uq", UN, "uint16")
+_buf("lu", 4 * UN, "uint16", UN)
+_buf("shelfs", 8192, "bfloat16")
+_buf("Xo Xq Xs Xf V VT sg tk S0A u ks kss yo qs w2", UN, "float32", CW)
+_buf("zi zm ci cj", UN, "int32", CW)
+_buf("off", UN, "uint16", CW)
+_buf("gv mx mn", NC * EW, "bfloat16", 256)
+_buf("B1 B2 B3 B4", UN, "bfloat16", CW)
+_buf("RD", 4 * UN, "bfloat16", CW)
+_buf("lq ly", 4 * UN, "float32", UN)
+_buf("KM Kc", UN, "float32")
+_buf("cmp", 6 * UN, "bfloat16", UN)
+_buf("cmps", 6 * UN, "bfloat16")
+_buf("sj", UN, "bfloat16")
+_buf("acc", 16, "float32", 1)
+_buf("R1 R2", 12, "uint16")
+_buf("Acol", 1, "float32")
+_buf("mmax mmin", EW, "bfloat16")
+_buf("rkm", 6 * UN, "bfloat16")
+_buf("m16 diag uf", UN, "float32")
+_buf("it", UN, "bfloat16")
+_buf("on1", CW, "bfloat16")
+_buf("nhalf", 128, "bfloat16")
+_buf("mm mi mG", 128, "float32")
+_buf("ic", 24, "int32", 1)
+_buf("fc", 72, "float32", 1)
+_buf("SG TR L EQ I16 Lh Eh TRl", 128, "float32")
+for _r in "12":
+    for _n in ("M0", "M1", "Y1", "DP", "SW", "SGX", "EQX", "EQl", "PG"):
+        _buf(_n + _r, 128, "float32")
+    _buf("TWp%s TWn%s" % (_r, _r), 128, "bfloat16")
+_buf("L2 L3 L4 I2 I3 I4", 128, "float32")
+_buf("AW1 AW2 AW3 AW4 KWp KWn QWp QWn", 128, "bfloat16")
+_buf("ZL ZH", 224, "bfloat16")
+_buf("pS0 pS1 pS2 pY0 pY1 pY2 pA pB", 512, "float32", None, "psum")
+PSUM = {n for n in SCRATCH if SCRATCH[n][0] == "psum"}
+SCRATCH["st"] = ("dram", [4, 128, 2048], "bfloat16")
+SCRATCH["rv"] = ("dram", [4, 128, 2048], "bfloat16")
+
+NDMA = 24
+SEMAPHORES = (["cv", "cs", "ct", "cg", "lo", "au", "ad", "aq", "ay"] + ["as%d" % a for a in range(4)]
+              + ["d%d" % k for k in range(NDMA)])
+
+
+def rank_program(g, core, T, topo):
+    rank = T.rank_of(core)
+    if rank is None:
+        return
+    j = rank % 4
+    quad = [T.cores[rank - j + a] for a in range(4)]
+    peers = [j ^ 1, j ^ 2, j ^ 3]
+
+    QUEUE = {"v": g.vector, "s": g.scalar, "t": g.tensor, "g": g, "y": g.sync}
+    SEM = {"v": "cv", "s": "cs", "t": "ct", "g": "cg"}
+    count = {}
+    known = {q: {} for q in QUEUE}
+    state = {}
+
+    def need(q, tok):
+        sem, n, who, clock = tok
+        if known[q].get(sem, 0) >= n:
+            return
+        QUEUE[q].wait_ge(T.sem[sem], n)
+        for s_, v_ in clock.items():
+            if known[q].get(s_, 0) < v_:
+                known[q][s_] = v_
+        known[q][sem] = n
+
+    def entry(k):
+        return state.setdefault(k, {"w": None, "r": {}})
+
+    def emit(q, call, reads=(), writes=(), dma=None):
+        toks = []
+        for ref in reads:
+            for k in ref[1]:
+                e = entry(k)
+                if k[0] in PSUM:
+                    toks += [t for t in e["r"].values() if t[2] != q]
+                if e["w"] and not (k[0] in PSUM and q == "t"):
+                    toks.append(e["w"])
+        for ref in writes:
+            for k in ref[1]:
+                e = entry(k)
+                if k[0] in PSUM:
+                    toks += [t for t in e["r"].values() if t[2] != q or q != "t"]
+                else:
+                    if e["w"]:
+                        toks.append(e["w"])
+                    toks += list(e["r"].values())
+        toks.sort(key=lambda t: -t[1])
+        for t in toks:
+            need(q, t)
+        sem = dma if dma else SEM[q]
+        inc = 16 if dma else 1
+        call().then_inc(T.sem[sem], inc)
+        count[sem] = count.get(sem, 0) + inc
+        tok = (sem, count[sem], None if dma else q, dict(known[q]))
+        for ref in reads:
+            for k in ref[1]:
+                state[k]["r"][sem] = tok
+        for ref in writes:
+            for k in ref[1]:
+                if k[0] in PSUM:
+                    state[k]["r"][sem] = tok
+                    state[k]["w"] = None if q == "t" else tok
+                else:
+                    state[k] = {"w": tok, "r": {}}
+        return tok
+
+    def A(name, lo=0, hi=None, step=None, p0=0, p1=128):
+        hi = SCRATCH[name][1][1] if hi is None else hi
+        ap = T[name][p0:p1, lo:hi] if step is None else T[name][p0:p1, lo:hi:step]
+        gr = GRAN[name]
+        return (ap, [(name, k) for k in range(lo // gr, (hi - 1) // gr + 1)])
+
+    def ind(win, off):
+        return (win[0].indirect(off[0]), win[1] + off[1])
+
+    def val(x):
+        return x[0] if isinstance(x, tuple) else x
+
+    def refs(*xs):
+        return [x for x in xs if isinstance(x, tuple)]
+
+    def tt(out, a, b, op):
+        emit("v", lambda: g.vector.tensor_tensor(out=out[0], in0=a[0], in1=b[0], op=op), [a, b], [out])
+
+    def ts(out, a, s1, op0, s2=None, op1=None):
+        if op1 is None:
+            emit("v", lambda: g.vector.tensor_scalar(out=out[0], in0=a[0], scalar1=val(s1), scalar2=None, op0=op0),
+                 [a] + refs(s1), [out])
+        else:
+            emit("v", lambda: g.vector.tensor_scalar(out=out[0], in0=a[0], scalar1=val(s1), scalar2=val(s2), op0=op0, op1=op1),
+                 [a] + refs(s1, s2), [out])
+
+    def cp(out, a):
+        emit("v", lambda: g.vector.tensor_copy(out=out[0], in_=a[0]), [a], [out])
+
+    def scatter(win, off, a):
+        emit("v", lambda: g.vector.tensor_copy(out=win[0].indirect(off[0]), in_=a[0]), [a, off], [win])
+
+    def fill(out, x):
+        emit("v", lambda: g.vector.memset(out[0], x), [], [out])
+
+    def scan(out, a, b, init, op0, op1):
+        emit("v", lambda: g.vector.tensor_tensor_scan(out=out[0], data0=a[0], data1=b[0], initial=init, op0=op0, op1=op1),
+             [a, b], [out])
+
+    def act(out, a, func, bias=None, scale=None, acc=None):
+        kw = {}
+        if bias is not None:
+            kw["bias"] = val(bias)
+        if scale is not None:
+            kw["scale"] = val(scale)
+        if acc is not None:
+            kw["accum_out"] = acc[0]
+        emit("s", lambda: g.scalar.activation(out=out[0], in_=a[0], func=func, **kw), [a] + refs(bias, scale), [out] + refs(acc))
+
+    def mm(out, lhs, rhs, start=True, stop=True):
+        emit("t", lambda: g.tensor.matmul(out=out[0], lhsT=lhs[0], rhs=rhs[0], start=start, stop=stop), [lhs, rhs], [out])
+
+    ndma = [0]
+
+    def dma(q, out_ap, in_ap, reads=(), writes=()):
+        sem = "d%d" % ndma[0]
+        ndma[0] += 1
+        return emit(q, lambda: QUEUE[q].dma_start(out_ap, in_ap), reads, writes, dma=sem)
+
+    neng = len(topo.engines(core, quad[peers[0]]))
+
+    def fan(src, dst_name, sem):
+        for k in src[1]:
+            need("g", state[k]["w"])
+        ids = []
+        for a in peers:
+            rid, pid, _ = topo.addr(quad[a])
+            ids.append(DstId(rid=rid, pnc=pid))
+        dst = T[dst_name][:, UN * j:UN * j + UN]
+        g.remote_dma_fused([RemoteDMATransfer(dst_ids=ids, dma_engine_mask=topo.mask(core, quad[peers[0]]),
+                                              remote_sem=T.sem[sem], srcs=[src[0]], dsts=[dst, dst, dst])], local_sem=T.sem.lo)
+        count["lo"] = count.get("lo", 0) + neng
+
+    def landed(sem, n, keys):
+        count[sem] = n
+        for k in keys:
+            state[k] = {"w": (sem, n, None, {}), "r": {}}
+
+    def ic(k):
+        return A("ic", k, k + 1)
+
+    def fc(k):
+        return A("fc", k, k + 1)
+
+    dma("y", T.U32[:, :], T.units[:, :], [], [A("U32")])
+    dma("y", T.shelfs[:, :], T.shelf[:, :], [], [A("shelfs")])
+    stage = {}
+    for a in peers:
+        stage[a] = dma("y", T.st[a], T.shelf[32 * a:32 * a + 32, :])
+
+    def iota(ref, pattern, base=0, chan=0):
+        if ref[1][0][0] == "ic":
+            emit("g", lambda: g.iota(ref[0], pattern, base, chan), [], [ref])
+        else:
+            emit("g", lambda: g.iota(ref[0], pattern, base, chan, allow_small_or_imprecise_dtypes=True), [], [ref])
+
+    iota(ic(0), [[0, 1]], 0, 1)
+    iota(A("mi"), [[0, 8], [1, 16]])
+    iota(A("mG"), [[1, 8], [0, 16]])
+    iota(A("mm"), [[1, 128]])
+    cp(A("U16"), A("U32"))
+    fan(A("U16"), "lu", "au")
+    iota(A("uf"), [[0, 12], [1, 16]])
+    iota(A("it"), [[-2, UN]], -2)
+    ts(ic(1), ic(0), 15, ALU.bitwise_and)
+    ts(ic(2), ic(0), 4, ALU.logical_shift_right)
+    for k in range(7):
+        ts(ic(3 + k), ic(0), k, ALU.logical_shift_right, 1, ALU.bitwise_and)
+    cp(A("fc", 0, 10), A("ic", 0, 10))
+    P_, PI, PG_ = fc(0), fc(1), fc(2)
+    ts(A("Xo"), A("U32"), -BIG, ALU.add)
+    ts(A("SG"), A("mG"), PG_, ALU.is_equal)
+    ts(A("TR"), A("mi"), PI, ALU.is_ge)
+    tt(A("L"), A("SG"), A("TR"), ALU.mult)
+    ts(A("EQ"), A("mm"), P_, ALU.is_equal)
+    ts(A("I16"), A("EQ"), 16.0, ALU.mult)
+
+    def cc(name, c):
+        return A(name, CW * c, CW * c + CW)
+
+    def pS(c, k=0):
+        return A("pS%d" % c, CW * k, CW * k + CW)
+
+    def pT(c):
+        return pS(c, 1)
+
+    def pY(c):
+        return A("pY%d" % c, 0, CW)
+
+    def tail(c, mode):
+        if mode is None:
+            tt(cc("zi", c), pS(c), cc("S0A", c), ALU.add)
+        else:
+            ts(cc("zi", c), pS(c), mode, ALU.add)
+        yield
+        ts(cc("zm", c), cc("zi", c), 4095, ALU.bitwise_and)
+        yield
+        tt(cc("w2", c), cc("zm", c), cc("zm", c), ALU.mult)
+        yield
+        tt(cc("ci", c), cc("w2", c), pY(c), ALU.add)
+        yield
+        ts(cc("cj", c), cc("ci", c), 4, ALU.arith_shift_right, 8191, ALU.bitwise_and)
+        yield
+        cp(cc("off", c), cc("cj", c))
+
+    def run(*gens):
+        gens = list(gens)
+        while gens:
+            for x in list(gens):
+                if next(x, 1) == 1:
+                    gens.remove(x)
+
+    def ew(name, c, lo, hi):
+        return A(name, EW * c + 16 * lo, EW * c + 16 * hi)
+
+    def picks(c, lo, hi):
+        return ind(A("shelfs"), A("off", CW * c + lo, CW * c + hi))
+
+    def gather(c, lo=0, hi=CW):
+        act(ew("gv", c, lo, hi), picks(c, lo, hi), ACT.Copy)
+
+    def smax(c, lo=0, hi=CW):
+        scan(ew("mx", c, lo, hi), A("mmax", 0, 16 * (hi - lo)), ew("gv", c, lo, hi), 0.0, ALU.mult, ALU.max)
+
+    def smin(c, lo=0, hi=CW):
+        scan(ew("mn", c, lo, hi), A("mmin", 0, 16 * (hi - lo)), ew("gv", c, lo, hi), 0.0, ALU.add, ALU.min)
+
+    def last(name, c):
+        return A(name, EW * c + 15, EW * c + EW, 16)
+
+    def sums_first(ls, ly, X):
+        for bank, l, c in ((pS, ls, 0), (pS, ls, 1), (pY, ly, 0), (pY, ly, 1), (pS, ls, 2), (pY, ly, 2)):
+            mm(bank(c), l, cc(X, c))
+
+    def measure(X, mode, after):
+        sums_first(A("L"), A("I16"), X)
+        run(tail(0, mode), tail(1, mode))
+        run(tail(2, mode))
+        yield
+        gather(0)
+        gather(1)
+        gather(2, VG, CW)
+        cp(ew("gv", 2, 0, VG), picks(2, 0, VG))
+        smax(2, 0, VG)
+        smin(2, 0, VG)
+        for c in range(2):
+            smax(c)
+            smin(c)
+            after(c)
+        smax(2, VG, CW)
+        smin(2, VG, CW)
+        after(2)
+
+    def mask_fill(name, one, at, step, n):
+        fill(A(name), one)
+        fill(A(name, 0, n, step), at)
+
+    mask_fill("mmax", 1.0, 0.0, 16, EW)
+    mask_fill("mmin", 0.0, 512.0, 16, EW)
+
+    def ranges(c):
+        tt(A("RD", UN * j + CW * c, UN * j + CW * c + CW), last("mx", c), last("mn", c), ALU.subtract)
+
+    m1 = measure("Xo", 0.0, ranges)
+    next(m1)
+
+    def bits(base):
+        return A("fc", base, base + 7)
+    ts(bits(10), bits(3), -1.0, ALU.mult, 1.0, ALU.add)
+    ts(bits(17), bits(3), -2.0, ALU.mult, 1.0, ALU.add)
+    ts(bits(24), bits(3), 2.0, ALU.mult, -1.0, ALU.add)
+    ts(bits(31), bits(10), 16.0, ALU.mult)
+    ts(bits(38), bits(17), 448.0, ALU.mult)
+    ts(bits(45), bits(17), 512.0, ALU.mult)
+    ts(bits(52), bits(24), 512.0, ALU.mult)
+    HI1 = fc(6)
+    LOWC, L16, PBS = ({t: fc(b + 4 - t) for t in (1, 2, 3, 4)} for b in (10, 31, 24))
+    SIDE, NS, THR = ({r: fc(b + 4 + r) for r in (1, 2)} for b in (17, 24, 38))
+    K512, K512N = fc(52 + 6), fc(45 + 6)
+    Z0, Z15, H16, GB = fc(59), fc(60), fc(61), fc(66)
+    ts(Z0, PI, 0.0, ALU.is_equal, -1.0, ALU.mult)
+    ts(Z15, PI, 15.0, ALU.is_equal, fc(10 + 5), ALU.mult)
+    ts(GB, PG_, float(-2 * j), ALU.add)
+    ts(Z15, Z15, 8.0, ALU.mult)
+    ts(H16, HI1, 16.0, ALU.mult)
+    PX, GX = {}, {}
+    for r, X in ((1, 32), (2, 64)):
+        PX[r], GX[r] = fc(61 + r), fc(63 + r)
+        ts(PX[r], SIDE[r], float(X), ALU.mult, P_, ALU.add)
+        ts(GX[r], SIDE[r], X / 16.0, ALU.mult, PG_, ALU.add)
+    for name, x in (("ZL", -512.0), ("ZH", 512.0)):
+        fill(A(name), 0.0)
+        ts(A(name, 96, 128), A("mG", 0, 32), GB, ALU.is_equal, x, ALU.mult)
+    fill(A("on1"), 1.0)
+    ts(A("diag"), A("uf"), PI, ALU.is_equal)
+    mask_fill("m16", 1.0, 0.0, 16, UN)
+    mask_fill("rkm", 1.0, 0.0, UN, 6 * UN)
+    fill(A("nhalf"), -1.0 / 256)
+
+    def scaled(out, a, col):
+        act(A(out), A(a), ACT.Copy, scale=col)
+
+    for t in (2, 3, 4):
+        scaled("L%d" % t, "L", LOWC[t])
+        scaled("I%d" % t, "EQ", L16[t])
+    scaled("Lh", "L", HI1)
+    scaled("Eh", "EQ", H16)
+    scaled("TRl", "TR", LOWC[1])
+    scaled("KWp", "SG", K512)
+    scaled("KWn", "SG", K512N)
+    act(A("QWp"), A("SG"), ACT.Copy)
+    act(A("QWn"), A("SG"), ACT.Copy, scale=-1.0)
+
+    def pass_on(a):
+        need("g", stage[a])
+        rid, pid, _ = topo.addr(quad[a])
+        g.remote_dma(T.rv[j], T.st[a], T.sem["as%d" % j], T.sem.lo, pid, rid, topo.mask(core, quad[a]))
+        count["lo"] += neng
+
+    pass_on(peers[0])
+    pass_on(peers[1])
+    for _ in m1:
+        pass
+    fan(A("RD", UN * j, UN * j + UN), "RD", "ad")
+    pass_on(peers[2])
+
+    for r in (1, 2):
+        ts(A("SGX%d" % r), A("mG"), GX[r], ALU.is_equal)
+        ts(A("EQX%d" % r), A("mm"), PX[r], ALU.is_equal)
+        tt(A("PG%d" % r), A("SG"), A("SGX%d" % r), ALU.add)
+        ts(A("EQl%d" % r), A("EQX%d" % r), L16[1], ALU.mult)
+        tt(A("M0%d" % r), A("SGX%d" % r), A("TRl"), ALU.mult)
+        tt(A("Y1%d" % r), A("EQl%d" % r), A("Eh"), ALU.add)
+        tt(A("M1%d" % r), A("M0%d" % r), A("Lh"), ALU.add)
+        tt(A("DP%d" % r), A("EQX%d" % r), A("EQ"), ALU.subtract)
+        scaled("TWp%d" % r, "PG%d" % r, SIDE[r])
+        scaled("TWn%d" % r, "PG%d" % r, NS[r])
+        scaled("SW%d" % r, "PG%d" % r, Z0)
+        if r == 1:
+            scaled("AW1", "PG1", Z15)
+            for t in (2, 3, 4):
+                act(A("AW%d" % t), A("AW1"), ACT.Copy, scale=2.0 ** (1 - t))
+
+    landed("au", 3 * neng, [("lu", a) for a in peers])
+    for a in range(4):
+        if a == j:
+            src = A("U16", 0, UN, None, 32 * j, 32 * j + 32)
+        else:
+            src = A("lu", UN * a, UN * a + UN, None, 32 * j, 32 * j + 32)
+        dma("y", T.Uq[32 * a:32 * a + 32, :], src[0], [src], [(None, [("Uq4", a)])])
+    own_reads = list(state[("shelfs", 0)]["r"].values())
+    loads = []
+    for a in peers:
+        landed("as%d" % a, neng, [("rv", a)])
+        for t in own_reads:
+            need("y", t)
+        loads.append(dma("y", T.shelfs[32 * a:32 * a + 32, :], T.rv[a], [(None, [("rv", a)])], []))
+    ts(A("Xq"), (T.Uq[:, :], [("Uq4", a) for a in range(4)]), -BIG, ALU.add)
+
+    def iota_row(lo, hi):
+        mm(A("pA", lo, hi), A("nhalf"), A("it", lo, hi), True, False)
+
+    def sort(R):
+        tt(A("KM"), A("pA", 0, UN), A("diag"), ALU.mult)
+        act(A("ks"), A("pA", 0, UN), ACT.Copy)
+        scan(A("Kc"), A("m16"), A("KM"), 0.0, ALU.mult, ALU.add)
+
+        def key(k):
+            return A("Kc", 16 * k + 15, 16 * k + 16)
+        for k in range(6):
+            act(A("sj"), A("ks"), ACT.Sign, bias=key(k), scale=-1.0, acc=A("acc", k, k + 1))
+            ts(A("cmp", UN * k, UN * k + UN), A("ks"), key(6 + k), ALU.is_lt)
+        scan(A("cmps"), A("rkm"), A("cmp"), 0.0, ALU.mult, ALU.add)
+        cp(A(R, 6, 12), A("cmps", UN - 1, 6 * UN, UN))
+        ts(A(R, 0, 6), A("acc", 0, 6), 0.5, ALU.mult, 95.5, ALU.add)
+
+    ones = A("on1")
+
+    def search(r, R, mode, extra):
+        TWp, TWn = A("TWp%d" % r), A("TWn%d" % r)
+        scatter(A("Xs"), A(R), A("Xq"))
+        sums_first(A("M1%d" % r), A("Y1%d" % r), "Xs")
+        mm(A("pB", 0, UN), A("L"), A("Xs"))
+        mm(A("pA", 0, UN), A("DP%d" % r), A("Xs"))
+        if r == 1:
+            for tok in loads:
+                need("s", tok)
+        run(tail(0, mode), tail(1, mode))
+        run(tail(2, mode))
+        for c in range(NC):
+            gather(c)
+        scatter(A("kss"), A(R), A("ks"))
+        ts(A("S0A"), A("pB", 0, UN), mode, ALU.add)
+        cp(A("V"), A("pA", 0, UN))
+        mm(A("pA", UN, 2 * UN), A("SW%d" % r), A("kss"))
+
+        def rest():
+            extra()
+            cp(A("sg"), A("pA", UN, 2 * UN))
+            ts(A("tk"), A("sg"), NS[r], ALU.mult, THR[r], ALU.is_gt)
+
+        def sums(c):
+            mm(pT(c), A("nhalf"), ones, True, False)
+            mm(pT(c), TWp, last("mx", c), False, False)
+            mm(pT(c), TWn, last("mn", c), False, True)
+
+        def head(c, t):
+            tt(cc("u", c), pT(c), cc("sg", c), ALU.mult)
+            yield
+            bt = cc("B%d" % t, c) if r == 1 else pS(c, 2)
+            ts(bt, cc("u", c), PBS[t], ALU.mult, 0.0, ALU.is_gt)
+            yield
+            if t < 4:
+                tt(cc("V", c), bt, cc("V", c), ALU.mult)
+                mm(pS(c), A("L%d" % (t + 1)), cc("V", c))
+                mm(pY(c), A("I16"), cc("Xs", c), True, False)
+                mm(pY(c), A("I%d" % (t + 1)), cc("V", c), False, True)
+            else:
+                tt(pS(c, 3), bt, cc("VT", c), ALU.mult)
+                yield
+                tt(cc("Xf", c), pS(c, 3), cc("Xs", c), ALU.add)
+            yield
+
+        pend, pc = iter(()), None
+
+        for t in (1, 2, 3):
+            for c in range(NC):
+                smax(c)
+                next(pend, None)
+                smin(c)
+                sums(c)
+                if pc is None:
+                    rest()
+                for _ in range(4):
+                    next(pend, None)
+                h = head(c, t)
+                next(h)
+                next(pend, None)
+                if pc is not None:
+                    gather(pc)
+                next(h)
+                next(h)
+                if t == 3:
+                    tt(cc("VT", c), cc("tk", c), cc("V", c), ALU.mult)
+                pend, pc = tail(c, None), c
+        smax(0)
+        next(pend)
+        smin(0)
+        sums(0)
+        run(pend)
+        gather(pc)
+        h = head(0, 4)
+        for c in (1, 2):
+            next(h)
+            smax(c)
+            next(h)
+            smin(c)
+            sums(c)
+            next(h)
+            next(h)
+            h = head(c, 4)
+        next(h)
+        next(h)
+        if r == 1:
+            for t in (1, 2, 3, 4):
+                mm(A("pA", 0, UN), A("AW%d" % t), A("B%d" % t), t == 1, t == 4)
+        for _ in h:
+            pass
+
+    landed("ad", 3 * neng, [("RD", 3 * a + c) for a in peers for c in range(3)])
+    iota_row(0, UN)
+    for n, a in enumerate([j] + peers):
+        z = A("ZL" if a % 2 == 0 else "ZH", 96 - 32 * a, 224 - 32 * a)
+        mm(A("pA", 0, UN), z, A("RD", UN * a, UN * a + UN), False, n == 3)
+    sort("R1")
+    search(1, "R1", 0.0, lambda: None)
+    cp(A("Xq"), ind(A("Xf"), A("R1")))
+    emit("v", lambda: g.vector.tensor_reduce(out=T.Acol[:, :], in_=A("pA", 0, UN)[0], axis=AxisListType.X, op=ALU.add),
+         [A("pA", 0, UN)], [A("Acol")])
+
+    def keys2(c):
+        lo, hi = CW * c, CW * c + CW
+        iota_row(lo, hi)
+        mm(A("pA", lo, hi), A("KWp"), last("mx", c), False, False)
+        mm(A("pA", lo, hi), A("KWn"), last("mn", c), False, True)
+
+    for _ in measure("Xq", A("Acol"), keys2):
+        pass
+    sort("R2")
+    for c in range(NC):
+        q_ = A("pB", UN + CW * c, UN + CW * c + CW)
+        mm(q_, A("QWp"), last("mx", c), True, False)
+        mm(q_, A("QWn"), last("mn", c), False, True)
+
+    def send_q():
+        cp(A("qs"), A("pB", UN, 2 * UN))
+        fan(A("qs"), "lq", "aq")
+
+    search(2, "R2", A("Acol"), send_q)
+
+    landed("aq", 3 * neng, [("lq", a) for a in peers])
+    for a in [j] + peers:
+        lo = 0 if a == j else UN * a
+        name = "qs" if a == j else "lq"
+        src = A(name, lo, lo + UN)
+        dma("y", T.yq[2 * a:2 * a + 2, :], T[name][32 * j:32 * j + 32:16, lo:lo + UN], [src])
+    ts(A("yo"), ind(A("Xf"), A("R2")), BIG, ALU.add)
+    fan(A("yo"), "ly", "ay")
+    landed("ay", 3 * neng, [("ly", a) for a in peers])
+    for n, a in enumerate([j] + peers):
+        lo = 0 if a == j else UN * a
+        src = A("yo" if a == j else "ly", lo, lo + UN, None, 32 * j, 32 * j + 32)
+        dma("s" if n % 2 else "y", T.yu[32 * a:32 * a + 32, :], src[0], [src])
+    for sem, n in sorted(count.items()):
+        if known["y"].get(sem, 0) < n:
+            g.sync.wait_ge(T.sem[sem], n)

@@ -9,6 +9,8 @@ CW = 64
 EW = CW * 16
 VG = 32
 UN = 192
+STEP = "pabpcpDpphphp"
+PIECE = {"a": (0, CW // 2), "b": (CW // 2, CW), "c": (0, CW // 2), "D": (CW // 2, CW)}
 
 SCRATCH = {}
 GRAN = {}
@@ -476,68 +478,50 @@ def rank_program(g, core, T, topo):
             mm(pT(c), TWp, last("mx", c), False, False)
             mm(pT(c), TWn, last("mn", c), False, True)
 
-        def head(c, t):
+        def keep(c, t):
             tt(cc("u", c), pT(c), cc("sg", c), ALU.mult)
             yield
             bt = cc("B%d" % t, c) if r == 1 else pS(c, 2)
             ts(bt, cc("u", c), PBS[t], ALU.mult, 0.0, ALU.is_gt)
             yield
-            if t < 4:
-                tt(cc("V", c), bt, cc("V", c), ALU.mult)
-                mm(pS(c), A("L%d" % (t + 1)), cc("V", c))
-                mm(pY(c), A("I16"), cc("Xs", c), True, False)
-                mm(pY(c), A("I%d" % (t + 1)), cc("V", c), False, True)
-            else:
+            if t == 4:
                 tt(pS(c, 3), bt, cc("VT", c), ALU.mult)
                 yield
                 tt(cc("Xf", c), pS(c, 3), cc("Xs", c), ALU.add)
+                return
+            tt(cc("V", c), bt, cc("V", c), ALU.mult)
+            mm(pS(c), A("L%d" % (t + 1)), cc("V", c))
+            mm(pY(c), A("I16"), cc("Xs", c), True, False)
+            mm(pY(c), A("I%d" % (t + 1)), cc("V", c), False, True)
             yield
+            if t == 3:
+                tt(cc("VT", c), cc("tk", c), cc("V", c), ALU.mult)
+            for _ in tail(c, None):
+                yield
+            gather(c)
 
-        pend, pc = iter(()), None
-
-        for t in (1, 2, 3):
+        before = iter(())
+        for t in (1, 2, 3, 4):
             for c in range(NC):
-                smax(c)
-                next(pend, None)
-                smin(c)
-                sums(c)
-                if pc is None:
-                    rest()
-                for _ in range(4):
-                    next(pend, None)
-                h = head(c, t)
-                next(h)
-                next(pend, None)
-                if pc is not None:
-                    gather(pc)
-                next(h)
-                next(h)
-                if t == 3:
-                    tt(cc("VT", c), cc("tk", c), cc("V", c), ALU.mult)
-                pend, pc = tail(c, None), c
-        smax(0)
-        next(pend)
-        smin(0)
-        sums(0)
-        run(pend)
-        gather(pc)
-        h = head(0, 4)
-        for c in (1, 2):
-            next(h)
-            smax(c)
-            next(h)
-            smin(c)
-            sums(c)
-            next(h)
-            next(h)
-            h = head(c, 4)
-        next(h)
-        next(h)
+                now = keep(c, t)
+                for x in STEP:
+                    if x == "p":
+                        next(before, None)
+                    elif x == "h":
+                        if rest:
+                            rest()
+                            rest = None
+                        next(now)
+                    else:
+                        (smax if x in "ab" else smin)(c, *PIECE[x])
+                        if x == "D":
+                            sums(c)
+                run(before)
+                before = now
         if r == 1:
             for t in (1, 2, 3, 4):
                 mm(A("pA", 0, UN), A("AW%d" % t), A("B%d" % t), t == 1, t == 4)
-        for _ in h:
-            pass
+        run(before)
 
     landed("ad", 3 * neng, [("RD", 3 * a + c) for a in peers for c in range(3)])
     iota_row(0, UN)

from concourse.bass import DstId, RemoteDMATransfer
from concourse.mybir import AluOpType, AxisListType, ActivationFunctionType

ALU = AluOpType
ACT = ActivationFunctionType
BIG = float(1 << 19)
NC = 3
CW = 64
EW = CW * 16
VG = 32
UN = 192
STEP = "pabpcpDpphphp"
PIECE = {"a": (0, CW // 2), "b": (CW // 2, CW), "c": (0, CW // 2), "D": (CW // 2, CW)}

SCRATCH = {}
GRAN = {}


def _buf(names, cols, dtype, gran=None, where="sbuf"):
    for name in names.split():
        SCRATCH[name] = (where, [128, cols], dtype)
        GRAN[name] = gran if gran else cols


_buf("U32", UN, "int32")
_buf("U16 Uq", UN, "uint16")
_buf("lu", 4 * UN, "uint16", UN)
_buf("shelfs", 8192, "bfloat16")
_buf("Xo Xq Xs Xf V VT sg tk S0A u ks kss yo qs w2", UN, "float32", CW)
_buf("zi zm ci cj", UN, "int32", CW)
_buf("off", UN, "uint16", CW)
_buf("gv mx mn", NC * EW, "bfloat16", 256)
_buf("B1 B2 B3 B4", UN, "bfloat16", CW)
_buf("RD", 4 * UN, "bfloat16", CW)
_buf("lq ly", 4 * UN, "float32", UN)
_buf("KM Kc", UN, "float32")
_buf("cmp", 6 * UN, "bfloat16", UN)
_buf("cmps", 6 * UN, "bfloat16")
_buf("sj", UN, "bfloat16")
_buf("acc", 16, "float32", 1)
_buf("R1 R2", 12, "uint16")
_buf("Acol", 1, "float32")
_buf("mmax mmin", EW, "bfloat16")
_buf("rkm", 6 * UN, "bfloat16")
_buf("m16 diag uf", UN, "float32")
_buf("it", UN, "bfloat16")
_buf("on1", CW, "bfloat16")
_buf("nhalf", 128, "bfloat16")
_buf("mm mi mG", 128, "float32")
_buf("ic", 24, "int32", 1)
_buf("fc", 72, "float32", 1)
_buf("SG TR L EQ I16 Lh Eh TRl", 128, "float32")
for _r in "12":
    for _n in ("M0", "M1", "Y1", "DP", "SW", "SGX", "EQX", "EQl", "PG"):
        _buf(_n + _r, 128, "float32")
    _buf("TWp%s TWn%s" % (_r, _r), 128, "bfloat16")
_buf("L2 L3 L4 I2 I3 I4", 128, "float32")
_buf("AW1 AW2 AW3 AW4 KWp KWn QWp QWn", 128, "bfloat16")
_buf("ZL ZH", 224, "bfloat16")
_buf("pS0 pS1 pS2 pY0 pY1 pY2 pA pB", 512, "float32", None, "psum")
PSUM = {n for n in SCRATCH if SCRATCH[n][0] == "psum"}
SCRATCH["st"] = ("dram", [4, 128, 2048], "bfloat16")
SCRATCH["rv"] = ("dram", [4, 128, 2048], "bfloat16")

NDMA = 24
SEMAPHORES = (["cv", "cs", "ct", "cg", "lo", "au", "ad", "aq", "ay"] + ["as%d" % a for a in range(4)]
              + ["d%d" % k for k in range(NDMA)])


def rank_program(g, core, T, topo):
    rank = T.rank_of(core)
    if rank is None:
        return
    j = rank % 4
    quad = [T.cores[rank - j + a] for a in range(4)]
    peers = [j ^ 1, j ^ 2, j ^ 3]

    QUEUE = {"v": g.vector, "s": g.scalar, "t": g.tensor, "g": g, "y": g.sync}
    SEM = {"v": "cv", "s": "cs", "t": "ct", "g": "cg"}
    count = {}
    known = {q: {} for q in QUEUE}
    state = {}

    def need(q, tok):
        sem, n, who, clock = tok
        if known[q].get(sem, 0) >= n:
            return
        QUEUE[q].wait_ge(T.sem[sem], n)
        for s_, v_ in clock.items():
            if known[q].get(s_, 0) < v_:
                known[q][s_] = v_
        known[q][sem] = n

    def entry(k):
        return state.setdefault(k, {"w": None, "r": {}})

    def emit(q, call, reads=(), writes=(), dma=None):
        toks = []
        for ref in reads:
            for k in ref[1]:
                e = entry(k)
                if k[0] in PSUM:
                    toks += [t for t in e["r"].values() if t[2] != q]
                if e["w"] and not (k[0] in PSUM and q == "t"):
                    toks.append(e["w"])
        for ref in writes:
            for k in ref[1]:
                e = entry(k)
                if k[0] in PSUM:
                    toks += [t for t in e["r"].values() if t[2] != q or q != "t"]
                else:
                    if e["w"]:
                        toks.append(e["w"])
                    toks += list(e["r"].values())
        toks.sort(key=lambda t: -t[1])
        for t in toks:
            need(q, t)
        sem = dma if dma else SEM[q]
        inc = 16 if dma else 1
        call().then_inc(T.sem[sem], inc)
        count[sem] = count.get(sem, 0) + inc
        tok = (sem, count[sem], None if dma else q, dict(known[q]))
        for ref in reads:
            for k in ref[1]:
                state[k]["r"][sem] = tok
        for ref in writes:
            for k in ref[1]:
                if k[0] in PSUM:
                    state[k]["r"][sem] = tok
                    state[k]["w"] = None if q == "t" else tok
                else:
                    state[k] = {"w": tok, "r": {}}
        return tok

    def A(name, lo=0, hi=None, step=None, p0=0, p1=128):
        hi = SCRATCH[name][1][1] if hi is None else hi
        ap = T[name][p0:p1, lo:hi] if step is None else T[name][p0:p1, lo:hi:step]
        gr = GRAN[name]
        return (ap, [(name, k) for k in range(lo // gr, (hi - 1) // gr + 1)])

    def ind(win, off):
        return (win[0].indirect(off[0]), win[1] + off[1])

    def val(x):
        return x[0] if isinstance(x, tuple) else x

    def refs(*xs):
        return [x for x in xs if isinstance(x, tuple)]

    def tt(out, a, b, op):
        emit("v", lambda: g.vector.tensor_tensor(out=out[0], in0=a[0], in1=b[0], op=op), [a, b], [out])

    def ts(out, a, s1, op0, s2=None, op1=None):
        if op1 is None:
            emit("v", lambda: g.vector.tensor_scalar(out=out[0], in0=a[0], scalar1=val(s1), scalar2=None, op0=op0),
                 [a] + refs(s1), [out])
        else:
            emit("v", lambda: g.vector.tensor_scalar(out=out[0], in0=a[0], scalar1=val(s1), scalar2=val(s2), op0=op0, op1=op1),
                 [a] + refs(s1, s2), [out])

    def cp(out, a):
        emit("v", lambda: g.vector.tensor_copy(out=out[0], in_=a[0]), [a], [out])

    def scatter(win, off, a):
        emit("v", lambda: g.vector.tensor_copy(out=win[0].indirect(off[0]), in_=a[0]), [a, off], [win])

    def fill(out, x):
        emit("v", lambda: g.vector.memset(out[0], x), [], [out])

    def scan(out, a, b, init, op0, op1):
        emit("v", lambda: g.vector.tensor_tensor_scan(out=out[0], data0=a[0], data1=b[0], initial=init, op0=op0, op1=op1),
             [a, b], [out])

    def act(out, a, func, bias=None, scale=None, acc=None):
        kw = {}
        if bias is not None:
            kw["bias"] = val(bias)
        if scale is not None:
            kw["scale"] = val(scale)
        if acc is not None:
            kw["accum_out"] = acc[0]
        emit("s", lambda: g.scalar.activation(out=out[0], in_=a[0], func=func, **kw), [a] + refs(bias, scale), [out] + refs(acc))

    def mm(out, lhs, rhs, start=True, stop=True):
        emit("t", lambda: g.tensor.matmul(out=out[0], lhsT=lhs[0], rhs=rhs[0], start=start, stop=stop), [lhs, rhs], [out])

    ndma = [0]

    def dma(q, out_ap, in_ap, reads=(), writes=()):
        sem = "d%d" % ndma[0]
        ndma[0] += 1
        return emit(q, lambda: QUEUE[q].dma_start(out_ap, in_ap), reads, writes, dma=sem)

    neng = len(topo.engines(core, quad[peers[0]]))

    def fan(src, dst_name, sem):
        for k in src[1]:
            need("g", state[k]["w"])
        ids = []
        for a in peers:
            rid, pid, _ = topo.addr(quad[a])
            ids.append(DstId(rid=rid, pnc=pid))
        dst = T[dst_name][:, UN * j:UN * j + UN]
        g.remote_dma_fused([RemoteDMATransfer(dst_ids=ids, dma_engine_mask=topo.mask(core, quad[peers[0]]),
                                              remote_sem=T.sem[sem], srcs=[src[0]], dsts=[dst, dst, dst])], local_sem=T.sem.lo)
        count["lo"] = count.get("lo", 0) + neng

    def landed(sem, n, keys):
        count[sem] = n
        for k in keys:
            state[k] = {"w": (sem, n, None, {}), "r": {}}

    def ic(k):
        return A("ic", k, k + 1)

    def fc(k):
        return A("fc", k, k + 1)

    dma("y", T.U32[:, :], T.units[:, :], [], [A("U32")])
    dma("y", T.shelfs[:, :], T.shelf[:, :], [], [A("shelfs")])
    stage = {}
    for a in peers:
        stage[a] = dma("y", T.st[a], T.shelf[32 * a:32 * a + 32, :])

    def iota(ref, pattern, base=0, chan=0):
        if ref[1][0][0] == "ic":
            emit("g", lambda: g.iota(ref[0], pattern, base, chan), [], [ref])
        else:
            emit("g", lambda: g.iota(ref[0], pattern, base, chan, allow_small_or_imprecise_dtypes=True), [], [ref])

    iota(ic(0), [[0, 1]], 0, 1)
    iota(A("mi"), [[0, 8], [1, 16]])
    iota(A("mG"), [[1, 8], [0, 16]])
    iota(A("mm"), [[1, 128]])
    cp(A("U16"), A("U32"))
    fan(A("U16"), "lu", "au")
    iota(A("uf"), [[0, 12], [1, 16]])
    iota(A("it"), [[-2, UN]], -2)
    ts(ic(1), ic(0), 15, ALU.bitwise_and)
    ts(ic(2), ic(0), 4, ALU.logical_shift_right)
    for k in range(7):
        ts(ic(3 + k), ic(0), k, ALU.logical_shift_right, 1, ALU.bitwise_and)
    cp(A("fc", 0, 10), A("ic", 0, 10))
    P_, PI, PG_ = fc(0), fc(1), fc(2)
    ts(A("Xo"), A("U32"), -BIG, ALU.add)
    ts(A("SG"), A("mG"), PG_, ALU.is_equal)
    ts(A("TR"), A("mi"), PI, ALU.is_ge)
    tt(A("L"), A("SG"), A("TR"), ALU.mult)
    ts(A("EQ"), A("mm"), P_, ALU.is_equal)
    ts(A("I16"), A("EQ"), 16.0, ALU.mult)

    def cc(name, c):
        return A(name, CW * c, CW * c + CW)

    def pS(c, k=0):
        return A("pS%d" % c, CW * k, CW * k + CW)

    def pT(c):
        return pS(c, 1)

    def pY(c):
        return A("pY%d" % c, 0, CW)

    def tail(c, mode):
        if mode is None:
            tt(cc("zi", c), pS(c), cc("S0A", c), ALU.add)
        else:
            ts(cc("zi", c), pS(c), mode, ALU.add)
        yield
        ts(cc("zm", c), cc("zi", c), 4095, ALU.bitwise_and)
        yield
        tt(cc("w2", c), cc("zm", c), cc("zm", c), ALU.mult)
        yield
        tt(cc("ci", c), cc("w2", c), pY(c), ALU.add)
        yield
        ts(cc("cj", c), cc("ci", c), 4, ALU.arith_shift_right, 8191, ALU.bitwise_and)
        yield
        cp(cc("off", c), cc("cj", c))

    def run(*gens):
        gens = list(gens)
        while gens:
            for x in list(gens):
                if next(x, 1) == 1:
                    gens.remove(x)

    def ew(name, c, lo, hi):
        return A(name, EW * c + 16 * lo, EW * c + 16 * hi)

    def picks(c, lo, hi):
        return ind(A("shelfs"), A("off", CW * c + lo, CW * c + hi))

    def gather(c, lo=0, hi=CW):
        act(ew("gv", c, lo, hi), picks(c, lo, hi), ACT.Copy)

    def smax(c, lo=0, hi=CW):
        scan(ew("mx", c, lo, hi), A("mmax", 0, 16 * (hi - lo)), ew("gv", c, lo, hi), 0.0, ALU.mult, ALU.max)

    def smin(c, lo=0, hi=CW):
        scan(ew("mn", c, lo, hi), A("mmin", 0, 16 * (hi - lo)), ew("gv", c, lo, hi), 0.0, ALU.add, ALU.min)

    def last(name, c):
        return A(name, EW * c + 15, EW * c + EW, 16)

    def sums_first(ls, ly, X):
        for bank, l, c in ((pS, ls, 0), (pS, ls, 1), (pY, ly, 0), (pY, ly, 1), (pS, ls, 2), (pY, ly, 2)):
            mm(bank(c), l, cc(X, c))

    def measure(X, mode, after):
        sums_first(A("L"), A("I16"), X)
        run(tail(0, mode), tail(1, mode))
        run(tail(2, mode))
        yield
        gather(0)
        gather(1)
        gather(2, VG, CW)
        cp(ew("gv", 2, 0, VG), picks(2, 0, VG))
        smax(2, 0, VG)
        smin(2, 0, VG)
        for c in range(2):
            smax(c)
            smin(c)
            after(c)
        smax(2, VG, CW)
        smin(2, VG, CW)
        after(2)

    def mask_fill(name, one, at, step, n):
        fill(A(name), one)
        fill(A(name, 0, n, step), at)

    mask_fill("mmax", 1.0, 0.0, 16, EW)
    mask_fill("mmin", 0.0, 512.0, 16, EW)

    def ranges(c):
        tt(A("RD", UN * j + CW * c, UN * j + CW * c + CW), last("mx", c), last("mn", c), ALU.subtract)

    m1 = measure("Xo", 0.0, ranges)
    next(m1)

    def bits(base):
        return A("fc", base, base + 7)
    ts(bits(10), bits(3), -1.0, ALU.mult, 1.0, ALU.add)
    ts(bits(17), bits(3), -2.0, ALU.mult, 1.0, ALU.add)
    ts(bits(24), bits(3), 2.0, ALU.mult, -1.0, ALU.add)
    ts(bits(31), bits(10), 16.0, ALU.mult)
    ts(bits(38), bits(17), 448.0, ALU.mult)
    ts(bits(45), bits(17), 512.0, ALU.mult)
    ts(bits(52), bits(24), 512.0, ALU.mult)
    HI1 = fc(6)
    LOWC, L16, PBS = ({t: fc(b + 4 - t) for t in (1, 2, 3, 4)} for b in (10, 31, 24))
    SIDE, NS, THR = ({r: fc(b + 4 + r) for r in (1, 2)} for b in (17, 24, 38))
    K512, K512N = fc(52 + 6), fc(45 + 6)
    Z0, Z15, H16, GB = fc(59), fc(60), fc(61), fc(66)
    ts(Z0, PI, 0.0, ALU.is_equal, -1.0, ALU.mult)
    ts(Z15, PI, 15.0, ALU.is_equal, fc(10 + 5), ALU.mult)
    ts(GB, PG_, float(-2 * j), ALU.add)
    ts(Z15, Z15, 8.0, ALU.mult)
    ts(H16, HI1, 16.0, ALU.mult)
    PX, GX = {}, {}
    for r, X in ((1, 32), (2, 64)):
        PX[r], GX[r] = fc(61 + r), fc(63 + r)
        ts(PX[r], SIDE[r], float(X), ALU.mult, P_, ALU.add)
        ts(GX[r], SIDE[r], X / 16.0, ALU.mult, PG_, ALU.add)
    for name, x in (("ZL", -512.0), ("ZH", 512.0)):
        fill(A(name), 0.0)
        ts(A(name, 96, 128), A("mG", 0, 32), GB, ALU.is_equal, x, ALU.mult)
    fill(A("on1"), 1.0)
    ts(A("diag"), A("uf"), PI, ALU.is_equal)
    mask_fill("m16", 1.0, 0.0, 16, UN)
    mask_fill("rkm", 1.0, 0.0, UN, 6 * UN)
    fill(A("nhalf"), -1.0 / 256)

    def scaled(out, a, col):
        act(A(out), A(a), ACT.Copy, scale=col)

    for t in (2, 3, 4):
        scaled("L%d" % t, "L", LOWC[t])
        scaled("I%d" % t, "EQ", L16[t])
    scaled("Lh", "L", HI1)
    scaled("Eh", "EQ", H16)
    scaled("TRl", "TR", LOWC[1])
    scaled("KWp", "SG", K512)
    scaled("KWn", "SG", K512N)
    act(A("QWp"), A("SG"), ACT.Copy)
    act(A("QWn"), A("SG"), ACT.Copy, scale=-1.0)

    def pass_on(a):
        need("g", stage[a])
        rid, pid, _ = topo.addr(quad[a])
        g.remote_dma(T.rv[j], T.st[a], T.sem["as%d" % j], T.sem.lo, pid, rid, topo.mask(core, quad[a]))
        count["lo"] += neng

    pass_on(peers[0])
    pass_on(peers[1])
    for _ in m1:
        pass
    fan(A("RD", UN * j, UN * j + UN), "RD", "ad")
    pass_on(peers[2])

    for r in (1, 2):
        ts(A("SGX%d" % r), A("mG"), GX[r], ALU.is_equal)
        ts(A("EQX%d" % r), A("mm"), PX[r], ALU.is_equal)
        tt(A("PG%d" % r), A("SG"), A("SGX%d" % r), ALU.add)
        ts(A("EQl%d" % r), A("EQX%d" % r), L16[1], ALU.mult)
        tt(A("M0%d" % r), A("SGX%d" % r), A("TRl"), ALU.mult)
        tt(A("Y1%d" % r), A("EQl%d" % r), A("Eh"), ALU.add)
        tt(A("M1%d" % r), A("M0%d" % r), A("Lh"), ALU.add)
        tt(A("DP%d" % r), A("EQX%d" % r), A("EQ"), ALU.subtract)
        scaled("TWp%d" % r, "PG%d" % r, SIDE[r])
        scaled("TWn%d" % r, "PG%d" % r, NS[r])
        scaled("SW%d" % r, "PG%d" % r, Z0)
        if r == 1:
            scaled("AW1", "PG1", Z15)
            for t in (2, 3, 4):
                act(A("AW%d" % t), A("AW1"), ACT.Copy, scale=2.0 ** (1 - t))

    landed("au", 3 * neng, [("lu", a) for a in peers])
    for a in range(4):
        if a == j:
            src = A("U16", 0, UN, None, 32 * j, 32 * j + 32)
        else:
            src = A("lu", UN * a, UN * a + UN, None, 32 * j, 32 * j + 32)
        dma("y", T.Uq[32 * a:32 * a + 32, :], src[0], [src], [(None, [("Uq4", a)])])
    own_reads = list(state[("shelfs", 0)]["r"].values())
    loads = []
    for a in peers:
        landed("as%d" % a, neng, [("rv", a)])
        for t in own_reads:
            need("y", t)
        loads.append(dma("y", T.shelfs[32 * a:32 * a + 32, :], T.rv[a], [(None, [("rv", a)])], []))
    ts(A("Xq"), (T.Uq[:, :], [("Uq4", a) for a in range(4)]), -BIG, ALU.add)

    def iota_row(lo, hi):
        mm(A("pA", lo, hi), A("nhalf"), A("it", lo, hi), True, False)

    def sort(R):
        tt(A("KM"), A("pA", 0, UN), A("diag"), ALU.mult)
        act(A("ks"), A("pA", 0, UN), ACT.Copy)
        scan(A("Kc"), A("m16"), A("KM"), 0.0, ALU.mult, ALU.add)

        def key(k):
            return A("Kc", 16 * k + 15, 16 * k + 16)
        for k in range(6):
            act(A("sj"), A("ks"), ACT.Sign, bias=key(k), scale=-1.0, acc=A("acc", k, k + 1))
            ts(A("cmp", UN * k, UN * k + UN), A("ks"), key(6 + k), ALU.is_lt)
        scan(A("cmps"), A("rkm"), A("cmp"), 0.0, ALU.mult, ALU.add)
        cp(A(R, 6, 12), A("cmps", UN - 1, 6 * UN, UN))
        ts(A(R, 0, 6), A("acc", 0, 6), 0.5, ALU.mult, 95.5, ALU.add)

    ones = A("on1")

    def search(r, R, mode, extra):
        TWp, TWn = A("TWp%d" % r), A("TWn%d" % r)
        scatter(A("Xs"), A(R), A("Xq"))
        sums_first(A("M1%d" % r), A("Y1%d" % r), "Xs")
        mm(A("pB", 0, UN), A("L"), A("Xs"))
        mm(A("pA", 0, UN), A("DP%d" % r), A("Xs"))
        if r == 1:
            for tok in loads:
                need("s", tok)
        run(tail(0, mode), tail(1, mode))
        run(tail(2, mode))
        for c in range(NC):
            gather(c)
        scatter(A("kss"), A(R), A("ks"))
        ts(A("S0A"), A("pB", 0, UN), mode, ALU.add)
        cp(A("V"), A("pA", 0, UN))
        mm(A("pA", UN, 2 * UN), A("SW%d" % r), A("kss"))

        def rest():
            extra()
            cp(A("sg"), A("pA", UN, 2 * UN))
            ts(A("tk"), A("sg"), NS[r], ALU.mult, THR[r], ALU.is_gt)

        def sums(c):
            mm(pT(c), A("nhalf"), ones, True, False)
            mm(pT(c), TWp, last("mx", c), False, False)
            mm(pT(c), TWn, last("mn", c), False, True)

        def keep(c, t):
            tt(cc("u", c), pT(c), cc("sg", c), ALU.mult)
            yield
            bt = cc("B%d" % t, c) if r == 1 else pS(c, 2)
            ts(bt, cc("u", c), PBS[t], ALU.mult, 0.0, ALU.is_gt)
            yield
            if t == 4:
                tt(pS(c, 3), bt, cc("VT", c), ALU.mult)
                yield
                tt(cc("Xf", c), pS(c, 3), cc("Xs", c), ALU.add)
                return
            tt(cc("V", c), bt, cc("V", c), ALU.mult)
            mm(pS(c), A("L%d" % (t + 1)), cc("V", c))
            mm(pY(c), A("I16"), cc("Xs", c), True, False)
            mm(pY(c), A("I%d" % (t + 1)), cc("V", c), False, True)
            yield
            if t == 3:
                tt(cc("VT", c), cc("tk", c), cc("V", c), ALU.mult)
            for _ in tail(c, None):
                yield
            gather(c)

        before = iter(())
        for t in (1, 2, 3, 4):
            for c in range(NC):
                now = keep(c, t)
                for x in STEP:
                    if x == "p":
                        next(before, None)
                    elif x == "h":
                        if rest:
                            rest()
                            rest = None
                        next(now)
                    else:
                        (smax if x in "ab" else smin)(c, *PIECE[x])
                        if x == "D":
                            sums(c)
                run(before)
                before = now
        if r == 1:
            for t in (1, 2, 3, 4):
                mm(A("pA", 0, UN), A("AW%d" % t), A("B%d" % t), t == 1, t == 4)
        run(before)

    landed("ad", 3 * neng, [("RD", 3 * a + c) for a in peers for c in range(3)])
    iota_row(0, UN)
    for n, a in enumerate([j] + peers):
        z = A("ZL" if a % 2 == 0 else "ZH", 96 - 32 * a, 224 - 32 * a)
        mm(A("pA", 0, UN), z, A("RD", UN * a, UN * a + UN), False, n == 3)
    sort("R1")
    search(1, "R1", 0.0, lambda: None)
    cp(A("Xq"), ind(A("Xf"), A("R1")))
    emit("v", lambda: g.vector.tensor_reduce(out=T.Acol[:, :], in_=A("pA", 0, UN)[0], axis=AxisListType.X, op=ALU.add),
         [A("pA", 0, UN)], [A("Acol")])

    def keys2(c):
        lo, hi = CW * c, CW * c + CW
        iota_row(lo, hi)
        mm(A("pA", lo, hi), A("KWp"), last("mx", c), False, False)
        mm(A("pA", lo, hi), A("KWn"), last("mn", c), False, True)

    for _ in measure("Xq", A("Acol"), keys2):
        pass
    sort("R2")
    for c in range(NC):
        q_ = A("pB", UN + CW * c, UN + CW * c + CW)
        mm(q_, A("QWp"), last("mx", c), True, False)
        mm(q_, A("QWn"), last("mn", c), False, True)

    def send_q():
        cp(A("qs"), A("pB", UN, 2 * UN))
        fan(A("qs"), "lq", "aq")

    search(2, "R2", A("Acol"), send_q)

    landed("aq", 3 * neng, [("lq", a) for a in peers])
    for a in [j] + peers:
        lo = 0 if a == j else UN * a
        name = "qs" if a == j else "lq"
        src = A(name, lo, lo + UN)
        dma("y", T.yq[2 * a:2 * a + 2, :], T[name][32 * j:32 * j + 32:16, lo:lo + UN], [src])
    ts(A("yo"), ind(A("Xf"), A("R2")), BIG, ALU.add)
    fan(A("yo"), "ly", "ay")
    landed("ay", 3 * neng, [("ly", a) for a in peers])
    for n, a in enumerate([j] + peers):
        lo = 0 if a == j else UN * a
        src = A("yo" if a == j else "ly", lo, lo + UN, None, 32 * j, 32 * j + 32)
        dma("s" if n % 2 else "y", T.yu[32 * a:32 * a + 32, :], src[0], [src])
    for sem, n in sorted(count.items()):
        if known["y"].get(sem, 0) < n:
            g.sync.wait_ge(T.sem[sem], n)
